import numpy as np
import ml_dtypes


def mxq(x, axis, fmt="e4m3"):
    dtype, down = {"e4m3": (ml_dtypes.float8_e4m3fn, 7), "e5m2": (ml_dtypes.float8_e5m2, 14)}[fmt]
    v = np.moveaxis(np.asarray(x, np.float32).astype(ml_dtypes.bfloat16).astype(np.float64), axis, -1)
    blocks = v.reshape(v.shape[:-1] + (-1, 32))
    amax = np.abs(blocks).max(-1, keepdims=True)
    byte = np.maximum(np.where(amax > 0, np.frexp(amax)[1] - 1 + 127, 0) - down, 1)
    scale = np.exp2(byte - 127.0)
    codes = (blocks / scale).astype(np.float32).astype(dtype).astype(np.float64)
    return np.moveaxis((codes * scale).reshape(v.shape), -1, axis)


WIDE = False


def mx_kscale(k):
    if not WIDE:
        return np.ones(k)
    levels = np.array([10, -10, 5, -5, 0])
    if k % 512:
        return np.exp2(np.random.permutation(np.resize(levels, k // 32))).repeat(32)
    a = np.empty((k // 512, 16))
    for p in range(k // 512):
        a[p, :8] = np.random.permutation(np.resize(levels, 8))
        for g in range(8):
            far = levels[np.abs(levels - a[p, g]) >= 10]
            a[p, g + 8] = far[np.random.randint(len(far))]
    return np.exp2(a.ravel()).repeat(32)


def f64(x):
    return np.asarray(x).astype(np.float64)


def striped(idx):
    return np.tile(idx.reshape(-1, 16).T, (8, 1)).astype(np.uint16)


def unstriped(offs):
    return offs[:16].T.reshape(-1).astype(np.int64)


def striped8(idx):
    return np.concatenate([x.reshape(-1, 16).T for x in idx]).astype(np.uint16)


def runs(offs, k):
    lists = np.stack([offs[16 * r : 16 * r + 16].T.reshape(-1) for r in range(8)]).astype(np.int64)
    return lists[np.arange(k) % 512 // 64]


def pack_weight(w):
    k, n = w.shape
    w = f64(np.asarray(w, np.float32).astype(ml_dtypes.bfloat16)).reshape(k // 32, 32, n)
    amax = np.abs(w).max(1)
    byte = np.clip(np.where(amax > 0, np.frexp(amax)[1] - 1 + 127 - 7, 1), 1, 254)
    scaled = (w * np.exp2(127.0 - byte)[:, None, :]).reshape(k, n).astype(np.float32)
    words = np.ascontiguousarray(scaled.reshape(k // 512, 128, 4, n).transpose(0, 1, 3, 2)).astype(ml_dtypes.float8_e4m3fn).view(np.uint8)
    return words, np.ascontiguousarray(byte.astype(np.uint8).reshape(k // 512, 16, n))


def unpack_weight(words, scales):
    g, p, n, _ = words.shape
    vals = np.ascontiguousarray(words).view(ml_dtypes.float8_e4m3fn).astype(np.float64) * np.repeat(np.exp2(scales.astype(np.float64) - 127.0), 8, axis=1)[..., None]
    return vals.transpose(0, 1, 3, 2).reshape(g * 512, n)


E2M1 = np.array([0.0, 0.5, 1.0, 1.5, 2.0, 3.0, 4.0, 6.0, -0.0, -0.5, -1.0, -1.5, -2.0, -3.0, -4.0, -6.0])


def pack_fp4(w):
    k, n = w.shape
    w = f64(np.asarray(w, np.float32).astype(ml_dtypes.bfloat16)).reshape(k // 32, 32, n)
    amax = np.abs(w).max(1)
    mant, ex = np.frexp(amax / 6.0)
    byte = np.clip(np.where(amax > 0, np.where(mant > 0.5, ex, ex - 1) + 127, 1), 1, 254)
    scaled = (w * np.exp2(127.0 - byte)[:, None, :]).reshape(k, n).astype(np.float32)
    c = np.ascontiguousarray(scaled.reshape(k // 512, 128, 4, n).transpose(0, 1, 3, 2)).astype(ml_dtypes.float4_e2m1fn).view(np.uint8) & 0xF
    words = (c[..., 0::2] | (c[..., 1::2] << 4)).reshape(k // 512, 128, 2 * n)
    return np.ascontiguousarray(words), np.ascontiguousarray(byte.astype(np.uint8).reshape(k // 512, 16, n))


def unpack_fp4(words, scales):
    g, _, n = scales.shape
    words = np.ascontiguousarray(words).reshape(g, 128, n, 2)
    nib = np.empty((g, 128, n, 4), np.uint8)
    nib[..., 0::2] = words & 0xF
    nib[..., 1::2] = words >> 4
    vals = E2M1[nib] * np.repeat(np.exp2(scales.astype(np.float64) - 127.0), 8, axis=1)[..., None]
    return vals.transpose(0, 1, 3, 2).reshape(g * 512, n)


def planes(y):
    n, m = y.shape
    v = y.astype(np.float32).astype(ml_dtypes.bfloat16).astype(np.float64).reshape(n // 32, 32, m)
    top = np.abs(v).max(1)
    byte = np.clip(np.where(top > 0, np.frexp(top)[1] - 1 + 127 - 7, 1), 1, 254)
    codes = (v * np.exp2(127.0 - byte)[:, None, :]).reshape(n, m).astype(np.float32).astype(ml_dtypes.float8_e4m3fn).view(np.uint8)
    words = codes.reshape(n // 512, 128, 4, m).transpose(0, 1, 3, 2)
    return np.ascontiguousarray(words), np.ascontiguousarray(byte.astype(np.uint8).reshape(n // 512, 16, m))


K, T, S, N, G, H, W = 512, 2048, 256, 512, 2048, 512, 128


def setup_inputs():
    n = np.random.standard_normal
    s = mx_kscale(K)[:, None]
    u = mx_kscale(K)
    packed_xT = pack_weight(n((K, T)) * s)
    packed_dT = pack_weight(n((K, G)) / s)
    packed_w1 = pack_fp4(n((H, N)) / np.sqrt(H) / u[:, None])
    perm = np.random.permutation(S)
    return {
        "x_words": packed_xT[0],
        "x_scales": packed_xT[1],
        "d_words": packed_dT[0],
        "d_scales": packed_dT[1],
        "gn": (np.random.uniform(0.5, 1.5, (H, 1)) * u[:, None]).astype(np.float32),
        "w1_words": packed_w1[0],
        "w1_scales": packed_w1[1],
        "offs": striped8(np.random.randint(0, T, (8, S))),
        "k1": striped8(np.random.randint(0, G, (8, H))),
        "n1": striped(np.random.permutation(S)),
        "n2": striped(np.random.permutation(S)),
        "n3": striped(perm[:W]),
        "n4": striped(perm[W:]),
    }


def reference(x_words, x_scales, d_words, d_scales, gn, w1_words, w1_scales, offs, k1, n1, n2, n3, n4):
    d_k1 = unpack_weight(d_words, d_scales)[np.arange(K)[:, None], runs(k1, K)]
    xq = unpack_weight(x_words, x_scales)[np.arange(K)[:, None], runs(offs, K)]
    h = 0.0625 * (d_k1.T @ xq)
    z = f64(gn) * (h[:, unstriped(n1)] - h[:, unstriped(n2)])
    h2 = unpack_fp4(w1_words, w1_scales).T @ mxq(z, 0, "e4m3")
    pa = h2[:, unstriped(n3)]
    pb = h2[:, unstriped(n4)]
    rb = pa - pb
    ra = 0.75 * (pa + pb)
    ds = np.zeros((N, S))
    ds[:, unstriped(n3)] = ra
    out = ds.copy()
    out[:, unstriped(n4)] = rb
    return (out,) + planes(out)

@@ -1,0 +1,188 @@
+from contextlib import ExitStack
+
+import concourse.mybir as mybir
+
+F32 = mybir.dt.float32
+BF16 = mybir.dt.bfloat16
+I32 = mybir.dt.int32
+U32 = mybir.dt.uint32
+U16 = mybir.dt.uint16
+U8 = mybir.dt.uint8
+FP8X4 = mybir.dt.float8_e4m3fn_x4
+FP4X4 = mybir.dt.float4_e2m1fn_x4
+ALU = mybir.AluOpType
+COPY = mybir.ActivationFunctionType.Copy
+
+P = 128
+PACK = 4
+T = 2048
+S = 256
+H = 512
+N = 512
+W = 128
+PIECES = ((0, 128), (128, 192), (192, 256))
+
+FLOPS = 2 * 512 * H * S + 2 * H * N * S
+
+
+def tile_picked_hpqgaphaar_none_po_kernel(
+    tc, x_words, x_scales, d_words, d_scales, gn, w1_words, w1_scales, offs, k1, n1, n2, n3, n4, out_0, out_1, out_2
+):
+    nc = tc.nc
+    with ExitStack() as ctx:
+        sb = ctx.enter_context(tc.tile_pool(name="sb", bufs=1))
+        ps = ctx.enter_context(tc.psum_pool(name="ps", bufs=1))
+
+        def load_list(name, src):
+            tile = sb.tile([P, src.shape[1]], U16, name=name)
+            nc.sync.dma_start(tile[:], src)
+            return tile
+
+        def load_words(name, src):
+            tile = sb.tile([P, T], U32, name=name)
+            nc.sync.dma_start(tile[:].bitcast(I32), src[0].rearrange("p c r -> p (c r)").bitcast(I32))
+            return tile
+
+        def load_scale_rows(name, src):
+            tile = sb.tile([P, T], U8, name=name)
+            nc.vector.memset(tile[:].bitcast(I32), 0)
+            nc.scalar.dma_start(tile[0:P:8, :].bitcast(I32), src[0].bitcast(I32))
+            return tile
+
+        k1_sb = load_list("k1_sb", k1)
+        offs_sb = load_list("offs_sb", offs)
+        xs_table = load_scale_rows("xs_table", x_scales)
+        ds_table = load_scale_rows("ds_table", d_scales)
+        d_table = load_words("d_table", d_words)
+        n1_sb = load_list("n1_sb", n1)
+        n2_sb = load_list("n2_sb", n2)
+        x_table = load_words("x_table", x_words)
+        n3_sb = load_list("n3_sb", n3)
+        n4_sb = load_list("n4_sb", n4)
+
+        gn_sb = sb.tile([P, PACK], F32)
+        nc.gpsimd.dma_start(gn_sb[:], gn.rearrange("(p t) o -> p (t o)", t=PACK))
+        w1_raw = sb.tile([P, 2 * N], U8)
+        nc.gpsimd.dma_start(w1_raw[:].bitcast(I32), w1_words[0].bitcast(I32))
+        w1s_raw = sb.tile([P, N], U8)
+        nc.gpsimd.memset(w1s_raw[:].bitcast(I32), 0)
+        for q in range(4):
+            nc.gpsimd.dma_start(w1s_raw[32 * q : 32 * q + 4, :].bitcast(I32), w1_scales[0][4 * q : 4 * q + 4, :].bitcast(I32))
+
+        gain = sb.tile([P, PACK], F32)
+        nc.scalar.activation(gain[:], gn_sb[:], COPY, scale=0.0625)
+        w1_dealt = sb.tile([P, 2 * N], U8, align_bytes=64)
+        nc.scalar.copy(
+            w1_dealt[:].bitcast(U16).rearrange("p (t m) -> p t m", t=PACK),
+            w1_raw[:].bitcast(U16).rearrange("p (m t) -> p t m", t=PACK),
+        )
+
+        planes = sb.tile([P, H + S], U8, align_bytes=64)
+        xs_picked = sb.tile([P, S], U8)
+        nc.vector.tensor_copy(xs_picked[:], xs_table[:].indirect(offs_sb[:]))
+        ds_picked = sb.tile([P, H], U8)
+        nc.vector.tensor_copy(ds_picked[:], ds_table[:].indirect(k1_sb[:]))
+        nc.vector.tensor_copy(planes[:, H:].bitcast(I32), xs_picked[:].bitcast(I32))
+        nc.vector.tensor_copy(
+            planes[:, :H].rearrange("p (t m) -> p t m", t=PACK),
+            ds_picked[:].rearrange("p (m t) -> p t m", t=PACK),
+        )
+        for c in range(1, 4):
+            nc.scalar.dma_start(planes[c:P:32, :].bitcast(I32), planes[8 * c : P : 32, :].bitcast(I32))
+
+        d_picked = sb.tile([P, H], U32)
+        nc.vector.tensor_copy(d_picked[:], d_table[:].indirect(k1_sb[:]))
+        d_dealt = sb.tile([P, H], U32, align_bytes=64, tag="reused")
+        nc.vector.tensor_copy(
+            d_dealt[:].rearrange("p (t c i) -> p c t i", t=PACK, i=4),
+            d_picked[:].rearrange("p (c i t) -> p c t i", t=PACK, i=4),
+        )
+        x_picked = sb.tile([P, S], U32, align_bytes=64)
+        nc.vector.tensor_copy(x_picked[:], x_table[:].indirect(offs_sb[:]))
+
+        h = []
+        for t in range(PACK):
+            cols = slice(P * t, P * (t + 1))
+            acc = ps.tile([P, S], F32, name=f"h_acc{t}", tag=f"bank{t}")
+            nc.tensor.matmul_mx(
+                out=acc[:],
+                lhsT=d_dealt[:, cols].bitcast(FP8X4),
+                lhsT_scale=planes[:, cols],
+                rhs=x_picked[:].bitcast(FP8X4),
+                rhs_scale=planes[:, H:],
+                start=True,
+                stop=True,
+            )
+            h_t = sb.tile([P, S], F32, name=f"h{t}")
+            nc.vector.tensor_scalar(h_t[:], acc[:], gain[:, t : t + 1], None, ALU.mult)
+            h.append(h_t)
+
+        w1s_dealt = sb.tile([P, N], U8, align_bytes=64)
+        nc.vector.tensor_copy(
+            w1s_dealt[:].rearrange("p (t m) -> p t m", t=PACK),
+            w1s_raw[:].rearrange("p (m t) -> p t m", t=PACK),
+        )
+        z_words = sb.tile([P, S], U32, align_bytes=64)
+        z_scales = sb.tile([P, S], U8, align_bytes=64)
+        h2 = [sb.tile([P, S], F32, name=f"h2_{t}") for t in range(PACK)]
+        early = sb.tile([P, 2, PACK * P], F32)
+        late = sb.tile([P, 2, PACK * P], F32, align_bytes=64, tag="reused")
+        for lo, hi in PIECES:
+            width = hi - lo
+            entries = slice(lo // 16, hi // 16)
+            fetched = early if lo < P else late
+            start = PACK * (lo % P)
+            a = fetched[:, 0, start : start + PACK * width].rearrange("p (t j) -> p t j", t=PACK)
+            b = fetched[:, 1, start : start + PACK * width].rearrange("p (t j) -> p t j", t=PACK)
+            for t in range(PACK):
+                nc.scalar.activation(a[:, t, :], h[t][:].indirect(n1_sb[:, entries]), COPY)
+                nc.scalar.activation(b[:, t, :], h[t][:].indirect(n2_sb[:, entries]), COPY)
+            z = sb.tile([P, width * PACK], BF16, name=f"z{lo}", align_bytes=64, tag="z")
+            nc.vector.tensor_tensor(
+                z[:].rearrange("p (c i t) -> p c t i", t=PACK, i=4),
+                a.rearrange("p t (c i) -> p c t i", i=4),
+                b.rearrange("p t (c i) -> p c t i", i=4),
+                ALU.subtract,
+            )
+            nc.vector.quantize_mx(out=z_words[:, lo:hi].bitcast(FP8X4), scales=z_scales[:, lo:hi], in_=z[:])
+            if hi % P:
+                continue
+            cols = slice(hi - P, hi)
+            for t in range(PACK):
+                acc = ps.tile([P, P], F32, name=f"h2_acc{t}_{lo}", tag=f"bank{t + PACK if lo < P else t}")
+                nc.tensor.matmul_mx(
+                    out=acc[:],
+                    lhsT=w1_dealt[:, 2 * P * t : 2 * P * (t + 1)].bitcast(FP4X4),
+                    lhsT_scale=w1s_dealt[:, P * t : P * (t + 1)],
+                    rhs=z_words[:, cols].bitcast(FP8X4),
+                    rhs_scale=z_scales[:, cols],
+                    start=True,
+                    stop=True,
+                )
+                nc.vector.tensor_copy(h2[t][:, cols], acc[:])
+
+        y_rows = out_0.rearrange("(p t) j -> p t j", t=PACK)
+        y_bf = sb.tile([P, S, PACK], BF16, align_bytes=64)
+        pairs = []
+        for t in range(PACK):
+            picked = sb.tile([P, 2, W], F32, name=f"picked{t}")
+            nc.scalar.activation(picked[:, 0, :], h2[t][:].indirect(n3_sb[:]), COPY)
+            nc.scalar.activation(picked[:, 1, :], h2[t][:].indirect(n4_sb[:]), COPY)
+            mixed = sb.tile([P, 2, W], F32, name=f"mixed{t}")
+            nc.vector.tensor_tensor(mixed[:, 0, :], picked[:, 0, :], picked[:, 1, :], ALU.add)
+            nc.vector.tensor_tensor(mixed[:, 1, :], picked[:, 0, :], picked[:, 1, :], ALU.subtract)
+            pairs.append(mixed)
+        for t in range(PACK):
+            y = sb.tile([P, S], F32, name=f"y{t}")
+            nc.scalar.activation(y[:].indirect(n3_sb[:]), pairs[t][:, 0, :], COPY, scale=0.75)
+            nc.scalar.activation(y[:].indirect(n4_sb[:]), pairs[t][:, 1, :], COPY)
+            nc.sync.dma_start(y_rows[:, t, :], y[:])
+            nc.vector.tensor_copy(y_bf[:, :, t], y[:])
+
+        y_words = sb.tile([P, S], U32, align_bytes=64)
+        y_scales = sb.tile([P, S], U8, align_bytes=64)
+        nc.vector.quantize_mx(out=y_words[:].bitcast(FP8X4), scales=y_scales[:], in_=y_bf[:].rearrange("p j t -> p (j t)"))
+        nc.sync.dma_start(out_1[0].rearrange("p c r -> p (c r)").bitcast(I32), y_words[:].bitcast(I32))
+        for q in range(4):
+            queue = nc.scalar if q % 2 == 0 else nc.sync
+            queue.dma_start(out_2[0][4 * q : 4 * q + 4, :].bitcast(I32), y_scales[32 * q : 32 * q + 4, :].bitcast(I32))

@@ -20,7 +20,6 @@ S = 256
 H = 512
 N = 512
 W = 128
-PIECES = ((0, 128), (128, 192), (192, 256))
 
 FLOPS = 2 * 512 * H * S + 2 * H * N * S
 
@@ -43,16 +42,18 @@ def tile_picked_hpqgaphaar_none_po_kernel(
             nc.sync.dma_start(tile[:].bitcast(I32), src[0].rearrange("p c r -> p (c r)").bitcast(I32))
             return tile
 
-        def load_scale_rows(name, src):
+        def load_scale_rows(name, src, clearer):
             tile = sb.tile([P, T], U8, name=name)
-            nc.vector.memset(tile[:].bitcast(I32), 0)
-            nc.scalar.dma_start(tile[0:P:8, :].bitcast(I32), src[0].bitcast(I32))
+            clearer.memset(tile[:].bitcast(I32), 0)
+            nc.sync.dma_start(tile[0:P:8, :].bitcast(I32), src[0].bitcast(I32))
             return tile
 
+        gn_sb = sb.tile([P, PACK], F32)
+        nc.scalar.dma_start(gn_sb[:], gn.rearrange("(p t) o -> p (t o)", t=PACK))
         k1_sb = load_list("k1_sb", k1)
+        ds_table = load_scale_rows("ds_table", d_scales, nc.gpsimd)
         offs_sb = load_list("offs_sb", offs)
-        xs_table = load_scale_rows("xs_table", x_scales)
-        ds_table = load_scale_rows("ds_table", d_scales)
+        xs_table = load_scale_rows("xs_table", x_scales, nc.vector)
         d_table = load_words("d_table", d_words)
         n1_sb = load_list("n1_sb", n1)
         n2_sb = load_list("n2_sb", n2)
@@ -60,39 +61,32 @@ def tile_picked_hpqgaphaar_none_po_kernel(
         n3_sb = load_list("n3_sb", n3)
         n4_sb = load_list("n4_sb", n4)
 
-        gn_sb = sb.tile([P, PACK], F32)
-        nc.gpsimd.dma_start(gn_sb[:], gn.rearrange("(p t) o -> p (t o)", t=PACK))
-        w1_raw = sb.tile([P, 2 * N], U8)
-        nc.gpsimd.dma_start(w1_raw[:].bitcast(I32), w1_words[0].bitcast(I32))
+        w1_raw = sb.tile([P, 2 * N], U8, tag="reused")
+        nc.sync.dma_start(w1_raw[:].bitcast(I32), w1_words[0].bitcast(I32))
         w1s_raw = sb.tile([P, N], U8)
         nc.gpsimd.memset(w1s_raw[:].bitcast(I32), 0)
         for q in range(4):
             nc.gpsimd.dma_start(w1s_raw[32 * q : 32 * q + 4, :].bitcast(I32), w1_scales[0][4 * q : 4 * q + 4, :].bitcast(I32))
 
-        gain = sb.tile([P, PACK], F32)
+        gain = sb.tile([P, PACK], F32, align_bytes=64, tag="gain")
         nc.scalar.activation(gain[:], gn_sb[:], COPY, scale=0.0625)
-        w1_dealt = sb.tile([P, 2 * N], U8, align_bytes=64)
-        nc.scalar.copy(
-            w1_dealt[:].bitcast(U16).rearrange("p (t m) -> p t m", t=PACK),
-            w1_raw[:].bitcast(U16).rearrange("p (m t) -> p t m", t=PACK),
-        )
 
-        planes = sb.tile([P, H + S], U8, align_bytes=64)
-        xs_picked = sb.tile([P, S], U8)
-        nc.vector.tensor_copy(xs_picked[:], xs_table[:].indirect(offs_sb[:]))
+        planes = sb.tile([P, H + S], U8, align_bytes=64, tag="planes")
         ds_picked = sb.tile([P, H], U8)
         nc.vector.tensor_copy(ds_picked[:], ds_table[:].indirect(k1_sb[:]))
-        nc.vector.tensor_copy(planes[:, H:].bitcast(I32), xs_picked[:].bitcast(I32))
         nc.vector.tensor_copy(
             planes[:, :H].rearrange("p (t m) -> p t m", t=PACK),
             ds_picked[:].rearrange("p (m t) -> p t m", t=PACK),
         )
+        xs_picked = sb.tile([P, S], U8)
+        nc.vector.tensor_copy(xs_picked[:], xs_table[:].indirect(offs_sb[:]))
+        nc.vector.tensor_copy(planes[:, H:].bitcast(I32), xs_picked[:].bitcast(I32))
         for c in range(1, 4):
             nc.scalar.dma_start(planes[c:P:32, :].bitcast(I32), planes[8 * c : P : 32, :].bitcast(I32))
 
         d_picked = sb.tile([P, H], U32)
         nc.vector.tensor_copy(d_picked[:], d_table[:].indirect(k1_sb[:]))
-        d_dealt = sb.tile([P, H], U32, align_bytes=64, tag="reused")
+        d_dealt = sb.tile([P, H], U32, align_bytes=64)
         nc.vector.tensor_copy(
             d_dealt[:].rearrange("p (t c i) -> p c t i", t=PACK, i=4),
             d_picked[:].rearrange("p (c i t) -> p c t i", t=PACK, i=4),
@@ -117,7 +111,12 @@ def tile_picked_hpqgaphaar_none_po_kernel(
             nc.vector.tensor_scalar(h_t[:], acc[:], gain[:, t : t + 1], None, ALU.mult)
             h.append(h_t)
 
-        w1s_dealt = sb.tile([P, N], U8, align_bytes=64)
+        w1_dealt = sb.tile([P, 2 * N], U8, align_bytes=64, tag="gain")
+        nc.vector.tensor_copy(
+            w1_dealt[:].rearrange("p (t m b) -> p t m b", t=PACK, b=2),
+            w1_raw[:].rearrange("p (m t b) -> p t m b", t=PACK, b=2),
+        )
+        w1s_dealt = sb.tile([P, N], U8, align_bytes=64, tag="planes")
         nc.vector.tensor_copy(
             w1s_dealt[:].rearrange("p (t m) -> p t m", t=PACK),
             w1s_raw[:].rearrange("p (m t) -> p t m", t=PACK),
@@ -125,31 +124,32 @@ def tile_picked_hpqgaphaar_none_po_kernel(
         z_words = sb.tile([P, S], U32, align_bytes=64)
         z_scales = sb.tile([P, S], U8, align_bytes=64)
         h2 = [sb.tile([P, S], F32, name=f"h2_{t}") for t in range(PACK)]
-        early = sb.tile([P, 2, PACK * P], F32)
-        late = sb.tile([P, 2, PACK * P], F32, align_bytes=64, tag="reused")
-        for lo, hi in PIECES:
-            width = hi - lo
-            entries = slice(lo // 16, hi // 16)
-            fetched = early if lo < P else late
-            start = PACK * (lo % P)
-            a = fetched[:, 0, start : start + PACK * width].rearrange("p (t j) -> p t j", t=PACK)
-            b = fetched[:, 1, start : start + PACK * width].rearrange("p (t j) -> p t j", t=PACK)
+        for half, slot in enumerate(("fetched", "reused")):
+            lo = half * P
+            cols = slice(lo, lo + P)
+            fetched = sb.tile([P, 2, PACK, P], F32, name=f"fetched{half}", tag=slot)
+            a, b = fetched[:, 0], fetched[:, 1]
+            parts = 1 + half
+            step = P // parts
             for t in range(PACK):
-                nc.scalar.activation(a[:, t, :], h[t][:].indirect(n1_sb[:, entries]), COPY)
-                nc.scalar.activation(b[:, t, :], h[t][:].indirect(n2_sb[:, entries]), COPY)
-            z = sb.tile([P, width * PACK], BF16, name=f"z{lo}", align_bytes=64, tag="z")
-            nc.vector.tensor_tensor(
-                z[:].rearrange("p (c i t) -> p c t i", t=PACK, i=4),
-                a.rearrange("p t (c i) -> p c t i", i=4),
-                b.rearrange("p t (c i) -> p c t i", i=4),
-                ALU.subtract,
+                width = step if t == PACK - 1 else P
+                for j in range(0, P, width):
+                    entries = slice((lo + j) // 16, (lo + j + width) // 16)
+                    nc.scalar.activation(a[:, t, j : j + width], h[t][:].indirect(n1_sb[:, entries]), COPY)
+                    nc.scalar.activation(b[:, t, j : j + width], h[t][:].indirect(n2_sb[:, entries]), COPY)
+            z = sb.tile([P, P, PACK], BF16, name=f"z{half}", align_bytes=64)
+            for j in range(0, P, step):
+                nc.vector.tensor_tensor(
+                    z[:, j : j + step, :].rearrange("p (c i) t -> p c t i", i=4),
+                    a[:, :, j : j + step].rearrange("p t (c i) -> p c t i", i=4),
+                    b[:, :, j : j + step].rearrange("p t (c i) -> p c t i", i=4),
+                    ALU.subtract,
+                )
+            nc.vector.quantize_mx(
+                out=z_words[:, cols].bitcast(FP8X4), scales=z_scales[:, cols], in_=z[:].rearrange("p j t -> p (j t)")
             )
-            nc.vector.quantize_mx(out=z_words[:, lo:hi].bitcast(FP8X4), scales=z_scales[:, lo:hi], in_=z[:])
-            if hi % P:
-                continue
-            cols = slice(hi - P, hi)
             for t in range(PACK):
-                acc = ps.tile([P, P], F32, name=f"h2_acc{t}_{lo}", tag=f"bank{t + PACK if lo < P else t}")
+                acc = ps.tile([P, P], F32, name=f"h2_acc{t}_{half}", tag=f"bank{t + PACK * (1 - half)}")
                 nc.tensor.matmul_mx(
                     out=acc[:],
                     lhsT=w1_dealt[:, 2 * P * t : 2 * P * (t + 1)].bitcast(FP4X4),
@@ -159,10 +159,13 @@ def tile_picked_hpqgaphaar_none_po_kernel(
                     start=True,
                     stop=True,
                 )
-                nc.vector.tensor_copy(h2[t][:, cols], acc[:])
+                if t == 0 and half == 1:
+                    nc.scalar.copy(h2[t][:, cols], acc[:])
+                else:
+                    nc.vector.tensor_copy(h2[t][:, cols], acc[:])
 
         y_rows = out_0.rearrange("(p t) j -> p t j", t=PACK)
-        y_bf = sb.tile([P, S, PACK], BF16, align_bytes=64)
+        y_bf = [sb.tile([P, P, PACK], BF16, name=f"y_bf{half}", align_bytes=64) for half in range(2)]
         pairs = []
         for t in range(PACK):
             picked = sb.tile([P, 2, W], F32, name=f"picked{t}")
@@ -177,11 +180,16 @@ def tile_picked_hpqgaphaar_none_po_kernel(
             nc.scalar.activation(y[:].indirect(n3_sb[:]), pairs[t][:, 0, :], COPY, scale=0.75)
             nc.scalar.activation(y[:].indirect(n4_sb[:]), pairs[t][:, 1, :], COPY)
             nc.sync.dma_start(y_rows[:, t, :], y[:])
-            nc.vector.tensor_copy(y_bf[:, :, t], y[:])
+            for half in range(2):
+                nc.vector.tensor_copy(y_bf[half][:, :, t], y[:, half * P : (half + 1) * P])
 
         y_words = sb.tile([P, S], U32, align_bytes=64)
         y_scales = sb.tile([P, S], U8, align_bytes=64)
-        nc.vector.quantize_mx(out=y_words[:].bitcast(FP8X4), scales=y_scales[:], in_=y_bf[:].rearrange("p j t -> p (j t)"))
+        for half in range(2):
+            cols = slice(half * P, (half + 1) * P)
+            nc.vector.quantize_mx(
+                out=y_words[:, cols].bitcast(FP8X4), scales=y_scales[:, cols], in_=y_bf[half][:].rearrange("p j t -> p (j t)")
+            )
         nc.sync.dma_start(out_1[0].rearrange("p c r -> p (c r)").bitcast(I32), y_words[:].bitcast(I32))
         for q in range(4):
             queue = nc.scalar if q % 2 == 0 else nc.sync

@@ -50,26 +50,27 @@ def tile_picked_hpqgaphaar_none_po_kernel(
 
         gn_sb = sb.tile([P, PACK], F32)
         nc.scalar.dma_start(gn_sb[:], gn.rearrange("(p t) o -> p (t o)", t=PACK))
+        w1_raw = sb.tile([P, 2 * N], U8)
+        nc.scalar.dma_start(w1_raw[:].bitcast(I32), w1_words[0].bitcast(I32))
         k1_sb = load_list("k1_sb", k1)
         ds_table = load_scale_rows("ds_table", d_scales, nc.gpsimd)
         offs_sb = load_list("offs_sb", offs)
         xs_table = load_scale_rows("xs_table", x_scales, nc.vector)
         d_table = load_words("d_table", d_words)
         n1_sb = load_list("n1_sb", n1)
-        n2_sb = load_list("n2_sb", n2)
         x_table = load_words("x_table", x_words)
+        n2_sb = load_list("n2_sb", n2)
         n3_sb = load_list("n3_sb", n3)
         n4_sb = load_list("n4_sb", n4)
 
-        w1_raw = sb.tile([P, 2 * N], U8, tag="reused")
-        nc.sync.dma_start(w1_raw[:].bitcast(I32), w1_words[0].bitcast(I32))
-        w1s_raw = sb.tile([P, N], U8)
-        nc.gpsimd.memset(w1s_raw[:].bitcast(I32), 0)
-        for q in range(4):
-            nc.gpsimd.dma_start(w1s_raw[32 * q : 32 * q + 4, :].bitcast(I32), w1_scales[0][4 * q : 4 * q + 4, :].bitcast(I32))
-
-        gain = sb.tile([P, PACK], F32, align_bytes=64, tag="gain")
+        gain = sb.tile([P, PACK], F32, tag="reused")
         nc.scalar.activation(gain[:], gn_sb[:], COPY, scale=0.0625)
+
+        w1_dealt = sb.tile([P, 2 * N], U8, align_bytes=64)
+        nc.scalar.copy(
+            w1_dealt[:].bitcast(U16).rearrange("p (t m) -> p t m", t=PACK),
+            w1_raw[:].bitcast(U16).rearrange("p (m t) -> p t m", t=PACK),
+        )
 
         planes = sb.tile([P, H + S], U8, align_bytes=64, tag="planes")
         ds_picked = sb.tile([P, H], U8)
@@ -78,11 +79,16 @@ def tile_picked_hpqgaphaar_none_po_kernel(
             planes[:, :H].rearrange("p (t m) -> p t m", t=PACK),
             ds_picked[:].rearrange("p (m t) -> p t m", t=PACK),
         )
-        xs_picked = sb.tile([P, S], U8)
+        xs_picked = sb.tile([P, S], U8, align_bytes=64, tag="bytes")
         nc.vector.tensor_copy(xs_picked[:], xs_table[:].indirect(offs_sb[:]))
         nc.vector.tensor_copy(planes[:, H:].bitcast(I32), xs_picked[:].bitcast(I32))
         for c in range(1, 4):
             nc.scalar.dma_start(planes[c:P:32, :].bitcast(I32), planes[8 * c : P : 32, :].bitcast(I32))
+
+        w1s_raw = sb.tile([P, N], U8, align_bytes=64, tag="bytes")
+        nc.gpsimd.memset(w1s_raw[:].bitcast(I32), 0)
+        for q in range(4):
+            nc.sync.dma_start(w1s_raw[32 * q : 32 * q + 4, :].bitcast(I32), w1_scales[0][4 * q : 4 * q + 4, :].bitcast(I32))
 
         d_picked = sb.tile([P, H], U32)
         nc.vector.tensor_copy(d_picked[:], d_table[:].indirect(k1_sb[:]))
@@ -111,11 +117,6 @@ def tile_picked_hpqgaphaar_none_po_kernel(
             nc.vector.tensor_scalar(h_t[:], acc[:], gain[:, t : t + 1], None, ALU.mult)
             h.append(h_t)
 
-        w1_dealt = sb.tile([P, 2 * N], U8, align_bytes=64, tag="gain")
-        nc.vector.tensor_copy(
-            w1_dealt[:].rearrange("p (t m b) -> p t m b", t=PACK, b=2),
-            w1_raw[:].rearrange("p (m t b) -> p t m b", t=PACK, b=2),
-        )
         w1s_dealt = sb.tile([P, N], U8, align_bytes=64, tag="planes")
         nc.vector.tensor_copy(
             w1s_dealt[:].rearrange("p (t m) -> p t m", t=PACK),
@@ -137,7 +138,7 @@ def tile_picked_hpqgaphaar_none_po_kernel(
                     entries = slice((lo + j) // 16, (lo + j + width) // 16)
                     nc.scalar.activation(a[:, t, j : j + width], h[t][:].indirect(n1_sb[:, entries]), COPY)
                     nc.scalar.activation(b[:, t, j : j + width], h[t][:].indirect(n2_sb[:, entries]), COPY)
-            z = sb.tile([P, P, PACK], BF16, name=f"z{half}", align_bytes=64)
+            z = sb.tile([P, P, PACK], BF16, name=f"z{half}", align_bytes=64, tag="bytes")
             for j in range(0, P, step):
                 nc.vector.tensor_tensor(
                     z[:, j : j + step, :].rearrange("p (c i) t -> p c t i", i=4),

@@ -52,12 +52,12 @@ def tile_picked_hpqgaphaar_none_po_kernel(
         nc.scalar.dma_start(gn_sb[:], gn.rearrange("(p t) o -> p (t o)", t=PACK))
         w1_raw = sb.tile([P, 2 * N], U8)
         nc.scalar.dma_start(w1_raw[:].bitcast(I32), w1_words[0].bitcast(I32))
-        k1_sb = load_list("k1_sb", k1)
-        ds_table = load_scale_rows("ds_table", d_scales, nc.gpsimd)
         offs_sb = load_list("offs_sb", offs)
-        xs_table = load_scale_rows("xs_table", x_scales, nc.vector)
-        d_table = load_words("d_table", d_words)
+        xs_table = load_scale_rows("xs_table", x_scales, nc.gpsimd)
+        k1_sb = load_list("k1_sb", k1)
         n1_sb = load_list("n1_sb", n1)
+        ds_table = load_scale_rows("ds_table", d_scales, nc.vector)
+        d_table = load_words("d_table", d_words)
         x_table = load_words("x_table", x_words)
         n2_sb = load_list("n2_sb", n2)
         n3_sb = load_list("n3_sb", n3)
@@ -73,15 +73,15 @@ def tile_picked_hpqgaphaar_none_po_kernel(
         )
 
         planes = sb.tile([P, H + S], U8, align_bytes=64, tag="planes")
-        ds_picked = sb.tile([P, H], U8)
+        xs_picked = sb.tile([P, S], U8)
+        nc.vector.tensor_copy(xs_picked[:], xs_table[:].indirect(offs_sb[:]))
+        ds_picked = sb.tile([P, H], U8, align_bytes=64, tag="bytes")
         nc.vector.tensor_copy(ds_picked[:], ds_table[:].indirect(k1_sb[:]))
+        nc.vector.tensor_copy(planes[:, H:].bitcast(I32), xs_picked[:].bitcast(I32))
         nc.vector.tensor_copy(
             planes[:, :H].rearrange("p (t m) -> p t m", t=PACK),
             ds_picked[:].rearrange("p (m t) -> p t m", t=PACK),
         )
-        xs_picked = sb.tile([P, S], U8, align_bytes=64, tag="bytes")
-        nc.vector.tensor_copy(xs_picked[:], xs_table[:].indirect(offs_sb[:]))
-        nc.vector.tensor_copy(planes[:, H:].bitcast(I32), xs_picked[:].bitcast(I32))
         for c in range(1, 4):
             nc.scalar.dma_start(planes[c:P:32, :].bitcast(I32), planes[8 * c : P : 32, :].bitcast(I32))
 
@@ -100,22 +100,27 @@ def tile_picked_hpqgaphaar_none_po_kernel(
         x_picked = sb.tile([P, S], U32, align_bytes=64)
         nc.vector.tensor_copy(x_picked[:], x_table[:].indirect(offs_sb[:]))
 
-        h = []
-        for t in range(PACK):
-            cols = slice(P * t, P * (t + 1))
-            acc = ps.tile([P, S], F32, name=f"h_acc{t}", tag=f"bank{t}")
+        def first_product(t, cols, bank):
+            width = cols.stop - cols.start
+            acc = ps.tile([P, width], F32, name=f"h_acc{t}_{cols.start}", tag=f"bank{bank}")
+            rows = slice(P * t, P * (t + 1))
             nc.tensor.matmul_mx(
                 out=acc[:],
-                lhsT=d_dealt[:, cols].bitcast(FP8X4),
-                lhsT_scale=planes[:, cols],
-                rhs=x_picked[:].bitcast(FP8X4),
-                rhs_scale=planes[:, H:],
+                lhsT=d_dealt[:, rows].bitcast(FP8X4),
+                lhsT_scale=planes[:, rows],
+                rhs=x_picked[:, cols].bitcast(FP8X4),
+                rhs_scale=planes[:, H + cols.start : H + cols.stop],
                 start=True,
                 stop=True,
             )
-            h_t = sb.tile([P, S], F32, name=f"h{t}")
-            nc.vector.tensor_scalar(h_t[:], acc[:], gain[:, t : t + 1], None, ALU.mult)
-            h.append(h_t)
+            return acc
+
+        h = [sb.tile([P, S], F32, name=f"h{t}") for t in range(PACK)]
+        left, right = slice(0, P), slice(P, S)
+        nc.vector.tensor_scalar(h[0][:, left], first_product(0, left, 0)[:], gain[:, 0:1], None, ALU.mult)
+        nc.scalar.activation(h[0][:, right], first_product(0, right, PACK)[:], COPY, scale=gain[:, 0:1])
+        for t in range(1, PACK):
+            nc.vector.tensor_scalar(h[t][:], first_product(t, slice(0, S), t)[:], gain[:, t : t + 1], None, ALU.mult)
 
         w1s_dealt = sb.tile([P, N], U8, align_bytes=64, tag="planes")
         nc.vector.tensor_copy(
@@ -124,7 +129,7 @@ def tile_picked_hpqgaphaar_none_po_kernel(
         )
         z_words = sb.tile([P, S], U32, align_bytes=64)
         z_scales = sb.tile([P, S], U8, align_bytes=64)
-        h2 = [sb.tile([P, S], F32, name=f"h2_{t}") for t in range(PACK)]
+        h2_acc = []
         for half, slot in enumerate(("fetched", "reused")):
             lo = half * P
             cols = slice(lo, lo + P)
@@ -160,10 +165,16 @@ def tile_picked_hpqgaphaar_none_po_kernel(
                     start=True,
                     stop=True,
                 )
-                if t == 0 and half == 1:
-                    nc.scalar.copy(h2[t][:, cols], acc[:])
-                else:
-                    nc.vector.tensor_copy(h2[t][:, cols], acc[:])
+                h2_acc.append(acc)
+
+        h2 = [sb.tile([P, S], F32, name=f"h2_{t}") for t in range(2)]
+        h2.append(sb.tile([P, S], F32, name="h2_2", align_bytes=64, tag="bytes"))
+        h2.append(sb.tile([P, S], F32, name="h2_3", tag="reused"))
+        for t in range(PACK):
+            nc.vector.tensor_copy(h2[t][:, left], h2_acc[t][:])
+        nc.scalar.copy(h2[0][:, right], h2_acc[PACK][:])
+        for t in range(1, PACK):
+            nc.vector.tensor_copy(h2[t][:, right], h2_acc[PACK + t][:])
 
         y_rows = out_0.rearrange("(p t) j -> p t j", t=PACK)
         y_bf = [sb.tile([P, P, PACK], BF16, name=f"y_bf{half}", align_bytes=64) for half in range(2)]

from contextlib import ExitStack

import concourse.mybir as mybir

F32 = mybir.dt.float32
BF16 = mybir.dt.bfloat16
I32 = mybir.dt.int32
U32 = mybir.dt.uint32
U16 = mybir.dt.uint16
U8 = mybir.dt.uint8
FP8X4 = mybir.dt.float8_e4m3fn_x4
FP4X4 = mybir.dt.float4_e2m1fn_x4
ALU = mybir.AluOpType
COPY = mybir.ActivationFunctionType.Copy

P = 128
PACK = 4
T = 2048
S = 256
H = 512
N = 512
W = 128

FLOPS = 2 * 512 * H * S + 2 * H * N * S


def tile_picked_hpqgaphaar_none_po_kernel(
    tc, x_words, x_scales, d_words, d_scales, gn, w1_words, w1_scales, offs, k1, n1, n2, n3, n4, out_0, out_1, out_2
):
    nc = tc.nc
    with ExitStack() as ctx:
        sb = ctx.enter_context(tc.tile_pool(name="sb", bufs=1))
        ps = ctx.enter_context(tc.psum_pool(name="ps", bufs=1))

        def load_list(name, src):
            tile = sb.tile([P, src.shape[1]], U16, name=name)
            nc.sync.dma_start(tile[:], src)
            return tile

        def load_words(name, src):
            tile = sb.tile([P, T], U32, name=name)
            nc.sync.dma_start(tile[:].bitcast(I32), src[0].rearrange("p c r -> p (c r)").bitcast(I32))
            return tile

        def load_scale_rows(name, src, clearer):
            tile = sb.tile([P, T], U8, name=name)
            clearer.memset(tile[:].bitcast(I32), 0)
            nc.sync.dma_start(tile[0:P:8, :].bitcast(I32), src[0].bitcast(I32))
            return tile

        gn_sb = sb.tile([P, PACK], F32)
        nc.scalar.dma_start(gn_sb[:], gn.rearrange("(p t) o -> p (t o)", t=PACK))
        w1_raw = sb.tile([P, 2 * N], U8)
        nc.scalar.dma_start(w1_raw[:].bitcast(I32), w1_words[0].bitcast(I32))
        offs_sb = load_list("offs_sb", offs)
        xs_table = load_scale_rows("xs_table", x_scales, nc.gpsimd)
        k1_sb = load_list("k1_sb", k1)
        n1_sb = load_list("n1_sb", n1)
        ds_table = load_scale_rows("ds_table", d_scales, nc.vector)
        d_table = load_words("d_table", d_words)
        x_table = load_words("x_table", x_words)
        n2_sb = load_list("n2_sb", n2)
        n3_sb = load_list("n3_sb", n3)
        n4_sb = load_list("n4_sb", n4)

        gain = sb.tile([P, PACK], F32, tag="reused")
        nc.scalar.activation(gain[:], gn_sb[:], COPY, scale=0.0625)

        w1_dealt = sb.tile([P, 2 * N], U8, align_bytes=64)
        nc.scalar.copy(
            w1_dealt[:].bitcast(U16).rearrange("p (t m) -> p t m", t=PACK),
            w1_raw[:].bitcast(U16).rearrange("p (m t) -> p t m", t=PACK),
        )

        planes = sb.tile([P, H + S], U8, align_bytes=64, tag="planes")
        xs_picked = sb.tile([P, S], U8)
        nc.vector.tensor_copy(xs_picked[:], xs_table[:].indirect(offs_sb[:]))
        ds_picked = sb.tile([P, H], U8, align_bytes=64, tag="bytes")
        nc.vector.tensor_copy(ds_picked[:], ds_table[:].indirect(k1_sb[:]))
        nc.vector.tensor_copy(planes[:, H:].bitcast(I32), xs_picked[:].bitcast(I32))
        nc.vector.tensor_copy(
            planes[:, :H].rearrange("p (t m) -> p t m", t=PACK),
            ds_picked[:].rearrange("p (m t) -> p t m", t=PACK),
        )
        for c in range(1, 4):
            nc.scalar.dma_start(planes[c:P:32, :].bitcast(I32), planes[8 * c : P : 32, :].bitcast(I32))

        w1s_raw = sb.tile([P, N], U8, align_bytes=64, tag="bytes")
        nc.gpsimd.memset(w1s_raw[:].bitcast(I32), 0)
        for q in range(4):
            nc.sync.dma_start(w1s_raw[32 * q : 32 * q + 4, :].bitcast(I32), w1_scales[0][4 * q : 4 * q + 4, :].bitcast(I32))

        d_picked = sb.tile([P, H], U32)
        nc.vector.tensor_copy(d_picked[:], d_table[:].indirect(k1_sb[:]))
        d_dealt = sb.tile([P, H], U32, align_bytes=64)
        nc.vector.tensor_copy(
            d_dealt[:].rearrange("p (t c i) -> p c t i", t=PACK, i=4),
            d_picked[:].rearrange("p (c i t) -> p c t i", t=PACK, i=4),
        )
        x_picked = sb.tile([P, S], U32, align_bytes=64)
        nc.vector.tensor_copy(x_picked[:], x_table[:].indirect(offs_sb[:]))

        def first_product(t, cols, bank):
            width = cols.stop - cols.start
            acc = ps.tile([P, width], F32, name=f"h_acc{t}_{cols.start}", tag=f"bank{bank}")
            rows = slice(P * t, P * (t + 1))
            nc.tensor.matmul_mx(
                out=acc[:],
                lhsT=d_dealt[:, rows].bitcast(FP8X4),
                lhsT_scale=planes[:, rows],
                rhs=x_picked[:, cols].bitcast(FP8X4),
                rhs_scale=planes[:, H + cols.start : H + cols.stop],
                start=True,
                stop=True,
            )
            return acc

        h = [sb.tile([P, S], F32, name=f"h{t}") for t in range(PACK)]
        left, right = slice(0, P), slice(P, S)
        nc.vector.tensor_scalar(h[0][:, left], first_product(0, left, 0)[:], gain[:, 0:1], None, ALU.mult)
        nc.scalar.activation(h[0][:, right], first_product(0, right, PACK)[:], COPY, scale=gain[:, 0:1])
        for t in range(1, PACK):
            nc.vector.tensor_scalar(h[t][:], first_product(t, slice(0, S), t)[:], gain[:, t : t + 1], None, ALU.mult)

        w1s_dealt = sb.tile([P, N], U8, align_bytes=64, tag="planes")
        nc.vector.tensor_copy(
            w1s_dealt[:].rearrange("p (t m) -> p t m", t=PACK),
            w1s_raw[:].rearrange("p (m t) -> p t m", t=PACK),
        )
        z_words = sb.tile([P, S], U32, align_bytes=64)
        z_scales = sb.tile([P, S], U8, align_bytes=64)
        h2_acc = []
        for half, slot in enumerate(("fetched", "reused")):
            lo = half * P
            cols = slice(lo, lo + P)
            fetched = sb.tile([P, 2, PACK, P], F32, name=f"fetched{half}", tag=slot)
            a, b = fetched[:, 0], fetched[:, 1]
            parts = 1 + half
            step = P // parts
            for t in range(PACK):
                width = step if t == PACK - 1 else P
                for j in range(0, P, width):
                    entries = slice((lo + j) // 16, (lo + j + width) // 16)
                    nc.scalar.activation(a[:, t, j : j + width], h[t][:].indirect(n1_sb[:, entries]), COPY)
                    nc.scalar.activation(b[:, t, j : j + width], h[t][:].indirect(n2_sb[:, entries]), COPY)
            z = sb.tile([P, P, PACK], BF16, name=f"z{half}", align_bytes=64, tag="bytes")
            for j in range(0, P, step):
                nc.vector.tensor_tensor(
                    z[:, j : j + step, :].rearrange("p (c i) t -> p c t i", i=4),
                    a[:, :, j : j + step].rearrange("p t (c i) -> p c t i", i=4),
                    b[:, :, j : j + step].rearrange("p t (c i) -> p c t i", i=4),
                    ALU.subtract,
                )
            nc.vector.quantize_mx(
                out=z_words[:, cols].bitcast(FP8X4), scales=z_scales[:, cols], in_=z[:].rearrange("p j t -> p (j t)")
            )
            for t in range(PACK):
                acc = ps.tile([P, P], F32, name=f"h2_acc{t}_{half}", tag=f"bank{t + PACK * (1 - half)}")
                nc.tensor.matmul_mx(
                    out=acc[:],
                    lhsT=w1_dealt[:, 2 * P * t : 2 * P * (t + 1)].bitcast(FP4X4),
                    lhsT_scale=w1s_dealt[:, P * t : P * (t + 1)],
                    rhs=z_words[:, cols].bitcast(FP8X4),
                    rhs_scale=z_scales[:, cols],
                    start=True,
                    stop=True,
                )
                h2_acc.append(acc)

        h2 = [sb.tile([P, S], F32, name=f"h2_{t}") for t in range(2)]
        h2.append(sb.tile([P, S], F32, name="h2_2", align_bytes=64, tag="bytes"))
        h2.append(sb.tile([P, S], F32, name="h2_3", tag="reused"))
        for t in range(PACK):
            nc.vector.tensor_copy(h2[t][:, left], h2_acc[t][:])
        nc.scalar.copy(h2[0][:, right], h2_acc[PACK][:])
        for t in range(1, PACK):
            nc.vector.tensor_copy(h2[t][:, right], h2_acc[PACK + t][:])

        y_rows = out_0.rearrange("(p t) j -> p t j", t=PACK)
        y_bf = [sb.tile([P, P, PACK], BF16, name=f"y_bf{half}", align_bytes=64) for half in range(2)]
        pairs = []
        for t in range(PACK):
            picked = sb.tile([P, 2, W], F32, name=f"picked{t}")
            nc.scalar.activation(picked[:, 0, :], h2[t][:].indirect(n3_sb[:]), COPY)
            nc.scalar.activation(picked[:, 1, :], h2[t][:].indirect(n4_sb[:]), COPY)
            mixed = sb.tile([P, 2, W], F32, name=f"mixed{t}")
            nc.vector.tensor_tensor(mixed[:, 0, :], picked[:, 0, :], picked[:, 1, :], ALU.add)
            nc.vector.tensor_tensor(mixed[:, 1, :], picked[:, 0, :], picked[:, 1, :], ALU.subtract)
            pairs.append(mixed)
        for t in range(PACK):
            y = sb.tile([P, S], F32, name=f"y{t}")
            nc.scalar.activation(y[:].indirect(n3_sb[:]), pairs[t][:, 0, :], COPY, scale=0.75)
            nc.scalar.activation(y[:].indirect(n4_sb[:]), pairs[t][:, 1, :], COPY)
            nc.sync.dma_start(y_rows[:, t, :], y[:])
            for half in range(2):
                nc.vector.tensor_copy(y_bf[half][:, :, t], y[:, half * P : (half + 1) * P])

        y_words = sb.tile([P, S], U32, align_bytes=64)
        y_scales = sb.tile([P, S], U8, align_bytes=64)
        for half in range(2):
            cols = slice(half * P, (half + 1) * P)
            nc.vector.quantize_mx(
                out=y_words[:, cols].bitcast(FP8X4), scales=y_scales[:, cols], in_=y_bf[half][:].rearrange("p j t -> p (j t)")
            )
        nc.sync.dma_start(out_1[0].rearrange("p c r -> p (c r)").bitcast(I32), y_words[:].bitcast(I32))
        for q in range(4):
            queue = nc.scalar if q % 2 == 0 else nc.sync
            queue.dma_start(out_2[0][4 * q : 4 * q + 4, :].bitcast(I32), y_scales[32 * q : 32 * q + 4, :].bitcast(I32))
